import numpy as np
import ml_dtypes


def mxq(x, axis, fmt="e4m3"):
    dtype, down = {"e4m3": (ml_dtypes.float8_e4m3fn, 7), "e5m2": (ml_dtypes.float8_e5m2, 14)}[fmt]
    v = np.moveaxis(np.asarray(x, np.float32).astype(ml_dtypes.bfloat16).astype(np.float64), axis, -1)
    blocks = v.reshape(v.shape[:-1] + (-1, 32))
    amax = np.abs(blocks).max(-1, keepdims=True)
    byte = np.maximum(np.where(amax > 0, np.frexp(amax)[1] - 1 + 127, 0) - down, 1)
    scale = np.exp2(byte - 127.0)
    codes = (blocks / scale).astype(np.float32).astype(dtype).astype(np.float64)
    return np.moveaxis((codes * scale).reshape(v.shape), -1, axis)


WIDE = False


def mx_kscale(k):
    if not WIDE:
        return np.ones(k)
    levels = np.array([10, -10, 5, -5, 0])
    if k % 512:
        return np.exp2(np.random.permutation(np.resize(levels, k // 32))).repeat(32)
    a = np.empty((k // 512, 16))
    for p in range(k // 512):
        a[p, :8] = np.random.permutation(np.resize(levels, 8))
        for g in range(8):
            far = levels[np.abs(levels - a[p, g]) >= 10]
            a[p, g + 8] = far[np.random.randint(len(far))]
    return np.exp2(a.ravel()).repeat(32)


def f64(x):
    return np.asarray(x).astype(np.float64)


def striped(idx):
    return np.tile(np.asarray(idx).reshape(-1, 16).T, (8, 1)).astype(np.uint16)


def unstriped(offs):
    return offs[:16].T.reshape(-1).astype(np.int64)


E2M1 = np.array([0.0, 0.5, 1.0, 1.5, 2.0, 3.0, 4.0, 6.0, -0.0, -0.5, -1.0, -1.5, -2.0, -3.0, -4.0, -6.0])


def pack_weight(w, fmt):
    k, n = w.shape
    w = f64(np.asarray(w, np.float32).astype(ml_dtypes.bfloat16)).reshape(k // 32, 32, n)
    amax = np.abs(w).max(1)
    if fmt == "e4m3":
        byte = np.frexp(amax)[1] - 1 + 127 - 7
    else:
        mant, ex = np.frexp(amax / 6.0)
        byte = np.where(mant > 0.5, ex, ex - 1) + 127
    byte = np.clip(np.where(amax > 0, byte, 1), 1, 254)
    scaled = (w * np.exp2(127.0 - byte)[:, None, :]).reshape(k, n).astype(np.float32)
    by_word = np.ascontiguousarray(scaled.reshape(k // 512, 128, 4, n).transpose(0, 1, 3, 2))
    if fmt == "e4m3":
        words = by_word.astype(ml_dtypes.float8_e4m3fn).view(np.uint8)
    else:
        c = by_word.astype(ml_dtypes.float4_e2m1fn).view(np.uint8) & 0xF
        words = (c[..., 0::2] | (c[..., 1::2] << 4)).reshape(k // 512, 128, 2 * n)
    return np.ascontiguousarray(words), np.ascontiguousarray(byte.astype(np.uint8).reshape(k // 512, 16, n))


def unpack_weight(words, scales, fmt):
    g, _, n = scales.shape
    words = np.ascontiguousarray(words).reshape(g, 128, n, -1)
    if fmt == "e4m3":
        vals = words.view(ml_dtypes.float8_e4m3fn).astype(np.float64)
    else:
        nib = np.empty((g, 128, n, 4), np.uint8)
        nib[..., 0::2] = words & 0xF
        nib[..., 1::2] = words >> 4
        vals = E2M1[nib]
    vals = vals * np.repeat(np.exp2(scales.astype(np.float64) - 127.0), 8, axis=1)[..., None]
    return vals.transpose(0, 1, 3, 2).reshape(g * 512, n)


D, T, I, Q, E, V = 512, 2048, 512, 128, 512, 16


def setup_inputs():
    n = np.random.standard_normal
    idx = np.random.permutation(T)[:I]
    fd = mx_kscale(D)
    fi = mx_kscale(I)
    ti = np.ones(T)
    ti[idx] = fi
    keysp = pack_weight(n((D, T)) / fd[:, None], "e4m3")
    return {
        "query": (n((D, Q)) * 0.8 / np.sqrt(D) * fd[:, None]).astype(np.float32),
        "keys_words": keysp[0],
        "keys_scales": keysp[1],
        "lam": (np.random.uniform(0.05, 0.12, (1, Q))).astype(np.float32),
        "width": (np.random.uniform(0.3, 0.8, (Q, 1))).astype(np.float32),
        "os": (np.random.uniform(4.0, 16.0, (1, I)) * fi).astype(np.float32),
        "vals": (n((E, T)) / ti).astype(np.float32),
        "floors": (n((Q, E)) * 1.5).astype(np.float32),
        "offs": striped(idx),
    }


def reference(query, keys_words, keys_scales, lam, width, os, vals, floors, offs):
    idx = unstriped(offs)
    keysu = unpack_weight(keys_words, keys_scales, "e4m3")
    keysidxg = keysu[:, idx]
    queryq = mxq(f64(query), 0, "e4m3")
    a0 = keysidxg.T @ queryq
    ag = a0.reshape(I, V, Q // V).sum(axis=2)
    ar = np.repeat(ag, Q // V, axis=1)
    s0 = a0 - ar * f64(lam)
    s = s0.T
    ce = (s - np.mean(s, axis=1, keepdims=True)) / f64(width)
    p = 1.0 / (np.square(ce) + 1.0)
    w = p / np.sum(p, axis=1, keepdims=True)
    wo1 = w * f64(os)
    wt1 = wo1.T
    vt1 = f64(vals)[:, idx].T
    wt1q = mxq(wt1, 0, "e4m3")
    vt1q = mxq(vt1, 0, "e4m3")
    o = wt1q.T @ vt1q
    y = np.maximum(o, f64(floors)) + np.minimum(o, f64(floors)) * 0.1
    return y

@@ -1,0 +1,210 @@
+from contextlib import ExitStack
+
+import concourse.mybir as mybir
+from concourse.masks import make_identity
+
+D, T, I, Q, E = 512, 2048, 512, 128, 512
+FLOPS = 2 * I * D * Q + 2 * Q * I * E
+
+F32 = mybir.dt.float32
+BF16 = mybir.dt.bfloat16
+I32 = mybir.dt.int32
+U32 = mybir.dt.uint32
+U16 = mybir.dt.uint16
+U8 = mybir.dt.uint8
+FP8X4 = mybir.dt.float8_e4m3fn_x4
+ALU = mybir.AluOpType
+ACT = mybir.ActivationFunctionType
+
+P = 128
+PACK = 4
+GROUP = 8
+TILES = I // P
+PLANES = E // P
+
+
+def tile_attend_beyondgroup_typical_atleast_kernel(
+    tc, query, keys_words, keys_scales, lam, width, slot_factor, vals, floors, offs, out
+):
+    nc = tc.nc
+    with ExitStack() as ctx:
+        sb = ctx.enter_context(tc.tile_pool(name="sb", bufs=1))
+        ps = ctx.enter_context(tc.psum_pool(name="ps", bufs=1))
+
+        offsets = sb.tile([P, I // 16], U16, name="offsets")
+        nc.sync.dma_start(offsets[:], offs)
+
+        lam_col = sb.tile([Q, 1], F32, name="lam_col", tag="big0")
+        width_col = sb.tile([Q, 1], F32, name="width_col", tag="big1")
+        factor4 = sb.tile([P, PACK], F32, name="factor4")
+        with nc.allow_non_contiguous_dma(reason="one value a partition"):
+            nc.sync.dma_start(lam_col[:], lam.rearrange("o q -> q o"))
+            nc.sync.dma_start(width_col[:], width)
+        nc.sync.dma_start(factor4[:], slot_factor.rearrange("o (p t) -> p (o t)", t=PACK))
+
+        key_bytes = sb.tile([P, T], U8, name="key_bytes", tag="big3")
+        nc.gpsimd.memset(key_bytes[:].bitcast(I32), 0)
+        for quad in range(4):
+            nc.scalar.dma_start(
+                key_bytes[32 * quad : 32 * quad + 4, :].bitcast(I32),
+                keys_scales[0, 4 * quad : 4 * quad + 4, :].bitcast(I32),
+            )
+        key_words = sb.tile([P, T], U32, name="key_words", tag="big4")
+        nc.sync.dma_start(
+            key_words[:].bitcast(I32), keys_words[0].rearrange("p n t -> p (n t)").bitcast(I32)
+        )
+        q_raw = sb.tile([P, PACK, Q], F32, name="q_raw", tag="big2")
+        nc.sync.dma_start(q_raw[:], query.rearrange("(p t) q -> p t q", t=PACK))
+        ident = sb.tile([P, P], F32, name="ident")
+        make_identity(nc, ident[:])
+        one = sb.tile([P, 1], F32, name="one")
+        nc.gpsimd.memset(one[:], 1.0)
+        warm = sb.tile([P, 1], F32, name="warm")
+        nc.scalar.activation(warm[:], one[:], ACT.Abs_reciprocal_sqrt)
+
+        q_grouped = sb.tile([P, Q, PACK], BF16, name="q_grouped", align_bytes=64)
+        nc.scalar.copy(q_grouped[:], q_raw[:].rearrange("p t q -> p q t"))
+        q_codes = sb.tile([P, Q], U32, name="q_codes", align_bytes=64)
+        q_scales = sb.tile([P, Q], U8, name="q_scales", align_bytes=64)
+        nc.vector.quantize_mx(
+            out=q_codes[:].bitcast(FP8X4), scales=q_scales[:], in_=q_grouped[:].rearrange("p q t -> p (q t)")
+        )
+
+        k_scales = sb.tile([P, I], U8, name="k_scales", align_bytes=64)
+        nc.vector.tensor_copy(k_scales[:], key_bytes[:].indirect(offsets[:]))
+        k_codes = sb.tile([P, I], U32, name="k_codes", align_bytes=64)
+        nc.vector.tensor_copy(k_codes[:], key_words[:].indirect(offsets[:]))
+
+        neg_lam = sb.tile([Q, 1], F32, name="neg_lam")
+        nc.vector.tensor_scalar(neg_lam[:], lam_col[:], -1.0, None, ALU.mult)
+        inv_width = sb.tile([Q, 1], F32, name="inv_width")
+        nc.vector.reciprocal(inv_width[:], width_col[:])
+        mean_scale = sb.tile([Q, 1], F32, name="mean_scale")
+        nc.vector.tensor_scalar(mean_scale[:], inv_width[:], -1.0 / I, None, ALU.mult)
+        lam_rows = ps.tile([P, Q], F32, name="lam_rows", tag="bank0")
+        nc.tensor.transpose(lam_rows[:], neg_lam[:].to_broadcast([P, P]), ident[:])
+        factor_rows = ps.tile([P, PACK, P], F32, name="factor_rows", tag="bank1")
+        for t in range(PACK):
+            nc.tensor.transpose(factor_rows[:, t, :], factor4[:, t : t + 1].to_broadcast([P, P]), ident[:])
+
+        val_planes = []
+        for j in range(PLANES):
+            plane = sb.tile([P, T], F32, name=f"val_plane{j}", tag=f"big{j}")
+            nc.sync.dma_start(plane[:], vals[j * P : (j + 1) * P, :])
+            val_planes.append(plane)
+        floor_sb = sb.tile([Q, E], F32, name="floor_sb", tag="big4")
+        nc.sync.dma_start(floor_sb[:], floors)
+
+        a0 = ps.tile([P, TILES, Q], F32, name="a0", tag="bank2")
+        for t in range(TILES):
+            cols = slice(t * P, (t + 1) * P)
+            nc.tensor.matmul_mx(
+                out=a0[:, t, :],
+                lhsT=k_codes[:, cols].bitcast(FP8X4),
+                lhsT_scale=k_scales[:, cols],
+                rhs=q_codes[:].bitcast(FP8X4),
+                rhs_scale=q_scales[:],
+                start=True,
+                stop=True,
+            )
+        group_sum = sb.tile([P, TILES, Q // GROUP], F32, name="group_sum", tag="pick0", align_bytes=64)
+        nc.vector.tensor_reduce(
+            group_sum[:].rearrange("p t v -> p (t v)"),
+            a0[:].rearrange("p t (v j) -> p (t v) j", j=GROUP),
+            mybir.AxisListType.X,
+            ALU.add,
+        )
+        a0_sb = sb.tile([P, TILES, Q], F32, name="a0_sb")
+        nc.scalar.copy(a0_sb[:], a0[:])
+        shift = sb.tile([P, TILES, Q], F32, name="shift")
+        nc.vector.tensor_tensor(
+            shift[:].rearrange("p t (v j) -> p t v j", j=GROUP),
+            group_sum[:].unsqueeze(3).to_broadcast([P, TILES, Q // GROUP, GROUP]),
+            lam_rows[:].rearrange("p (v j) -> p v j", j=GROUP).unsqueeze(1).to_broadcast([P, TILES, Q // GROUP, GROUP]),
+            ALU.mult,
+        )
+        score = ps.tile([Q, TILES, P], F32, name="score", tag="bank3")
+        for n, src in enumerate((a0_sb, shift)):
+            for t in range(TILES):
+                nc.tensor.matmul(
+                    score[:, t, :],
+                    src[:, t, :],
+                    ident[:],
+                    is_transpose=True,
+                    start=(n == 0 and t == 0),
+                    stop=(n == 1 and t == TILES - 1),
+                )
+        score_row = score[:].rearrange("p t s -> p (t s)")
+
+        unused = sb.tile([Q, I], F32, name="unused")
+        neg_mean = sb.tile([Q, 1], F32, name="neg_mean")
+        nc.scalar.activation(unused[:], score_row, ACT.Identity, scale=mean_scale[:], accum_out=neg_mean[:])
+        z_sq = sb.tile([Q, I], F32, name="z_sq")
+        nc.scalar.activation(z_sq[:], score_row, ACT.Square, bias=neg_mean[:], scale=inv_width[:])
+        root = sb.tile([Q, I], F32, name="root")
+        nc.scalar.activation(root[:], z_sq[:], ACT.Abs_reciprocal_sqrt, bias=1.0)
+        part = sb.tile([Q, I], F32, name="part", tag="pick2", align_bytes=64)
+        part_sum = sb.tile([Q, 1], F32, name="part_sum")
+        nc.scalar.activation(part[:], root[:], ACT.Square, accum_out=part_sum[:])
+        def turn_and_quantise(rows, name, bank):
+            words = rows[:].bitcast(F32)
+            turned = ps.tile([P, 2, P], F32, name=f"{name}_turned", tag=bank)
+            for u in range(2):
+                nc.tensor.transpose(turned[:, u, :], words[:, u : I // 2 : 2], ident[:])
+            grouped = sb.tile([P, P * PACK], BF16, name=f"{name}_grouped", align_bytes=64)
+            nc.scalar.copy(
+                grouped[:].bitcast(F32).rearrange("p (c u) -> p c u", u=2), turned[:].rearrange("p u c -> p c u")
+            )
+            codes = sb.tile([P, P], U32, name=f"{name}_codes", align_bytes=64)
+            scales = sb.tile([P, P], U8, name=f"{name}_scales", align_bytes=64)
+            nc.vector.quantize_mx(out=codes[:].bitcast(FP8X4), scales=scales[:], in_=grouped[:])
+            return codes, scales
+
+        v_ops = []
+
+        def pick_values(j):
+            picked = sb.tile([P, I], BF16, name=f"picked{j}", tag=f"pick{j}", align_bytes=64)
+            nc.vector.tensor_copy(picked[:], val_planes[j][:].indirect(offsets[:]))
+            v_ops.append(turn_and_quantise(picked, f"v{j}", f"bank{4 + j}"))
+
+        for j in range(2):
+            pick_values(j)
+
+        inv_sum = sb.tile([Q, 1], F32, name="inv_sum", tag="big1")
+        nc.vector.reciprocal(inv_sum[:], part_sum[:])
+        weight = sb.tile([Q, I], BF16, name="weight", align_bytes=64)
+        nc.vector.scalar_tensor_tensor(
+            weight[:].rearrange("q (s t) -> q s t", t=PACK),
+            part[:].rearrange("q (s t) -> q s t", t=PACK),
+            inv_sum[:],
+            factor_rows[:].rearrange("q t s -> q s t"),
+            ALU.mult,
+            ALU.mult,
+        )
+
+        w_codes, w_scales = turn_and_quantise(weight, "w", "bank0")
+
+        for j in range(2, PLANES):
+            pick_values(j)
+
+        for first, last, bank in ((0, PLANES - 1, "bank2"), (PLANES - 1, PLANES, "bank3")):
+            n = (last - first) * P
+            cols = slice(first * P, last * P)
+            acc = ps.tile([Q, n], F32, name=f"acc{first}", tag=bank)
+            for j in range(first, last):
+                nc.tensor.matmul_mx(
+                    out=acc[:, (j - first) * P : (j - first + 1) * P],
+                    lhsT=w_codes[:].bitcast(FP8X4),
+                    lhsT_scale=w_scales[:],
+                    rhs=v_ops[j][0][:].bitcast(FP8X4),
+                    rhs_scale=v_ops[j][1][:],
+                    start=True,
+                    stop=True,
+                )
+            below = sb.tile([Q, n], F32, name=f"below{first}", tag=f"big{3 - first}")
+            nc.vector.scalar_tensor_tensor(below[:], acc[:], 0.1, floor_sb[:, cols], ALU.mult, ALU.add)
+            above = sb.tile([Q, n], F32, name=f"above{first}")
+            nc.vector.scalar_tensor_tensor(above[:], floor_sb[:, cols], 0.1, acc[:], ALU.mult, ALU.add)
+            result = sb.tile([Q, n], F32, name=f"result{first}")
+            nc.vector.tensor_tensor(result[:], below[:], above[:], ALU.max)
+            nc.sync.dma_start(out[:, cols], result[:])

@@ -23,6 +23,10 @@ TILES = I // P
 PLANES = E // P
 
 
+HALF = I // 2
+HEAD = 512
+
+
 def tile_attend_beyondgroup_typical_atleast_kernel(
     tc, query, keys_words, keys_scales, lam, width, slot_factor, vals, floors, offs, out
 ):
@@ -33,178 +37,201 @@ def tile_attend_beyondgroup_typical_atleast_kernel(
 
         offsets = sb.tile([P, I // 16], U16, name="offsets")
         nc.sync.dma_start(offsets[:], offs)
+        q_raw = sb.tile([P, PACK, Q], F32, name="q_raw")
+        nc.sync.dma_start(q_raw[:], query.rearrange("(p t) q -> p t q", t=PACK))
+        val_planes = [sb.tile([P, T], F32, name=f"val_plane{j}", tag=f"big{j}", align_bytes=64) for j in range(PLANES)]
+        nc.sync.dma_start(val_planes[0][:, :HEAD], vals[0:P, :HEAD])
 
-        lam_col = sb.tile([Q, 1], F32, name="lam_col", tag="big0")
-        width_col = sb.tile([Q, 1], F32, name="width_col", tag="big1")
-        factor4 = sb.tile([P, PACK], F32, name="factor4")
-        with nc.allow_non_contiguous_dma(reason="one value a partition"):
-            nc.sync.dma_start(lam_col[:], lam.rearrange("o q -> q o"))
-            nc.sync.dma_start(width_col[:], width)
-        nc.sync.dma_start(factor4[:], slot_factor.rearrange("o (p t) -> p (o t)", t=PACK))
-
-        key_bytes = sb.tile([P, T], U8, name="key_bytes", tag="big3")
-        nc.gpsimd.memset(key_bytes[:].bitcast(I32), 0)
+        key_bytes = sb.tile([P, T], U8, name="key_bytes")
+        nc.vector.memset(key_bytes[:].bitcast(I32), 0)
         for quad in range(4):
-            nc.scalar.dma_start(
+            nc.sync.dma_start(
                 key_bytes[32 * quad : 32 * quad + 4, :].bitcast(I32),
                 keys_scales[0, 4 * quad : 4 * quad + 4, :].bitcast(I32),
             )
-        key_words = sb.tile([P, T], U32, name="key_words", tag="big4")
+        key_words = sb.tile([P, T], U32, name="key_words")
         nc.sync.dma_start(
             key_words[:].bitcast(I32), keys_words[0].rearrange("p n t -> p (n t)").bitcast(I32)
         )
-        q_raw = sb.tile([P, PACK, Q], F32, name="q_raw", tag="big2")
-        nc.sync.dma_start(q_raw[:], query.rearrange("(p t) q -> p t q", t=PACK))
+        lam_col = sb.tile([Q, 1], F32, name="lam_col")
+        width_col = sb.tile([Q, 1], F32, name="width_col")
+        factor4 = sb.tile([P, PACK], F32, name="factor4")
+        with nc.allow_non_contiguous_dma(reason="one value a partition"):
+            nc.sync.dma_start(lam_col[:], lam.rearrange("o q -> q o"))
+            nc.sync.dma_start(val_planes[0][:, HEAD:], vals[0:P, HEAD:])
+            nc.sync.dma_start(width_col[:], width)
+        nc.sync.dma_start(val_planes[1][:], vals[P : 2 * P, :])
+        nc.sync.dma_start(factor4[:], slot_factor.rearrange("o (p t) -> p (o t)", t=PACK))
+        for j in range(2, PLANES):
+            nc.sync.dma_start(val_planes[j][:], vals[j * P : (j + 1) * P, :])
+        floor_tiles = {}
+        for first, last in ((0, PLANES - 1), (PLANES - 1, PLANES)):
+            tile = sb.tile([Q, (last - first) * P], F32, name=f"floor{first}", tag=f"floor{first}", align_bytes=64)
+            nc.sync.dma_start(tile[:], floors[:, first * P : last * P])
+            floor_tiles[first] = tile
+
         ident = sb.tile([P, P], F32, name="ident")
         make_identity(nc, ident[:])
         one = sb.tile([P, 1], F32, name="one")
-        nc.gpsimd.memset(one[:], 1.0)
+        nc.vector.memset(one[:], 1.0)
         warm = sb.tile([P, 1], F32, name="warm")
         nc.scalar.activation(warm[:], one[:], ACT.Abs_reciprocal_sqrt)
 
+
         q_grouped = sb.tile([P, Q, PACK], BF16, name="q_grouped", align_bytes=64)
         nc.scalar.copy(q_grouped[:], q_raw[:].rearrange("p t q -> p q t"))
+        k_scales = sb.tile([P, I], U8, name="k_scales", align_bytes=64)
+        nc.vector.tensor_copy(k_scales[:], key_bytes[:].indirect(offsets[:]))
         q_codes = sb.tile([P, Q], U32, name="q_codes", align_bytes=64)
         q_scales = sb.tile([P, Q], U8, name="q_scales", align_bytes=64)
         nc.vector.quantize_mx(
             out=q_codes[:].bitcast(FP8X4), scales=q_scales[:], in_=q_grouped[:].rearrange("p q t -> p (q t)")
         )
+        a0 = []
+        for h in range(2):
+            k_codes = sb.tile([P, HALF], U32, name=f"k_codes{h}", align_bytes=64)
+            nc.vector.tensor_copy(k_codes[:], key_words[:].indirect(offsets[:, h * 16 : (h + 1) * 16]))
+            bank = ps.tile([P, 2, Q], F32, name=f"a0_{h}", tag=f"bank{1 + h}")
+            for t in range(2):
+                nc.tensor.matmul_mx(
+                    out=bank[:, t, :],
+                    lhsT=k_codes[:, t * P : (t + 1) * P].bitcast(FP8X4),
+                    lhsT_scale=k_scales[:, h * HALF + t * P : h * HALF + (t + 1) * P],
+                    rhs=q_codes[:].bitcast(FP8X4),
+                    rhs_scale=q_scales[:],
+                    start=True,
+                    stop=True,
+                )
+            a0.append(bank)
 
-        k_scales = sb.tile([P, I], U8, name="k_scales", align_bytes=64)
-        nc.vector.tensor_copy(k_scales[:], key_bytes[:].indirect(offsets[:]))
-        k_codes = sb.tile([P, I], U32, name="k_codes", align_bytes=64)
-        nc.vector.tensor_copy(k_codes[:], key_words[:].indirect(offsets[:]))
-
-        neg_lam = sb.tile([Q, 1], F32, name="neg_lam")
-        nc.vector.tensor_scalar(neg_lam[:], lam_col[:], -1.0, None, ALU.mult)
-        inv_width = sb.tile([Q, 1], F32, name="inv_width")
-        nc.vector.reciprocal(inv_width[:], width_col[:])
-        mean_scale = sb.tile([Q, 1], F32, name="mean_scale")
-        nc.vector.tensor_scalar(mean_scale[:], inv_width[:], -1.0 / I, None, ALU.mult)
         lam_rows = ps.tile([P, Q], F32, name="lam_rows", tag="bank0")
-        nc.tensor.transpose(lam_rows[:], neg_lam[:].to_broadcast([P, P]), ident[:])
-        factor_rows = ps.tile([P, PACK, P], F32, name="factor_rows", tag="bank1")
+        nc.tensor.transpose(lam_rows[:], lam_col[:].to_broadcast([P, P]), ident[:])
+
+        group_sum = []
+        for h in range(2):
+            sums = sb.tile([P, 2, Q // GROUP], F32, name=f"group_sum{h}", tag=f"sums{h}", align_bytes=64)
+            nc.vector.tensor_reduce(
+                sums[:].rearrange("p t v -> p (t v)"),
+                a0[h][:].rearrange("p t (v j) -> p (t v) j", j=GROUP),
+                mybir.AxisListType.X,
+                ALU.add,
+            )
+            group_sum.append(sums)
+        score = []
+        for h in range(2):
+            neg_a0 = sb.tile([P, 2, Q], F32, name=f"neg_a0_{h}")
+            nc.scalar.activation(neg_a0[:], a0[h][:], ACT.Copy, scale=-1.0)
+            shift = sb.tile([P, 2, Q], F32, name=f"shift{h}")
+            nc.vector.tensor_tensor(
+                shift[:].rearrange("p t (v j) -> p t v j", j=GROUP),
+                group_sum[h][:].unsqueeze(3).to_broadcast([P, 2, Q // GROUP, GROUP]),
+                lam_rows[:].rearrange("p (v j) -> p v j", j=GROUP).unsqueeze(1).to_broadcast([P, 2, Q // GROUP, GROUP]),
+                ALU.mult,
+            )
+            bank = ps.tile([Q, 2, P], F32, name=f"score{h}", tag=f"bank{3 + h}")
+            for n, src in enumerate((neg_a0, shift)):
+                for t in range(2):
+                    nc.tensor.matmul(
+                        bank[:, t, :], src[:, t, :], ident[:], is_transpose=True,
+                        start=(n == 0 and t == 0), stop=(n == 1 and t == 1),
+                    )
+            score.append(bank[:].rearrange("p t s -> p (t s)"))
+
+        width_sq = sb.tile([Q, 1], F32, name="width_sq")
+        nc.gpsimd.tensor_tensor(width_sq[:], width_col[:], width_col[:], ALU.mult)
+        unused = sb.tile([Q, I], F32, name="unused")
+        first_share = sb.tile([Q, 1], F32, name="first_share")
+        nc.scalar.activation(unused[:, :HALF], score[0], ACT.Identity, scale=-1.0 / (I * HALF), accum_out=first_share[:])
+        neg_mean = sb.tile([Q, 1], F32, name="neg_mean")
+        nc.scalar.activation(
+            unused[:, HALF:], score[1], ACT.Identity, bias=first_share[:], scale=-1.0 / I, accum_out=neg_mean[:]
+        )
+        z_sq = sb.tile([Q, I], F32, name="z_sq")
+        for h in range(2):
+            nc.scalar.activation(
+                z_sq[:, h * HALF : (h + 1) * HALF], score[h], ACT.Square, bias=neg_mean[:]
+            )
+        root = sb.tile([Q, I], F32, name="root", tag="root", align_bytes=64)
+        for h in range(2):
+            cols = slice(h * HALF, (h + 1) * HALF)
+            nc.scalar.activation(root[:, cols], z_sq[:, cols], ACT.Abs_reciprocal_sqrt, bias=width_sq[:])
+        part = sb.tile([Q, I], F32, name="part", tag="part", align_bytes=64)
+        part_sum = sb.tile([Q, 1], F32, name="part_sum")
+        nc.scalar.activation(part[:], root[:], ACT.Square, accum_out=part_sum[:])
+
+        factor_rows = ps.tile([P, PACK, P], F32, name="factor_rows", tag="bank0")
         for t in range(PACK):
             nc.tensor.transpose(factor_rows[:, t, :], factor4[:, t : t + 1].to_broadcast([P, P]), ident[:])
 
-        val_planes = []
-        for j in range(PLANES):
-            plane = sb.tile([P, T], F32, name=f"val_plane{j}", tag=f"big{j}")
-            nc.sync.dma_start(plane[:], vals[j * P : (j + 1) * P, :])
-            val_planes.append(plane)
-        floor_sb = sb.tile([Q, E], F32, name="floor_sb", tag="big4")
-        nc.sync.dma_start(floor_sb[:], floors)
-
-        a0 = ps.tile([P, TILES, Q], F32, name="a0", tag="bank2")
-        for t in range(TILES):
-            cols = slice(t * P, (t + 1) * P)
-            nc.tensor.matmul_mx(
-                out=a0[:, t, :],
-                lhsT=k_codes[:, cols].bitcast(FP8X4),
-                lhsT_scale=k_scales[:, cols],
-                rhs=q_codes[:].bitcast(FP8X4),
-                rhs_scale=q_scales[:],
-                start=True,
-                stop=True,
-            )
-        group_sum = sb.tile([P, TILES, Q // GROUP], F32, name="group_sum", tag="pick0", align_bytes=64)
-        nc.vector.tensor_reduce(
-            group_sum[:].rearrange("p t v -> p (t v)"),
-            a0[:].rearrange("p t (v j) -> p (t v) j", j=GROUP),
-            mybir.AxisListType.X,
-            ALU.add,
-        )
-        a0_sb = sb.tile([P, TILES, Q], F32, name="a0_sb")
-        nc.scalar.copy(a0_sb[:], a0[:])
-        shift = sb.tile([P, TILES, Q], F32, name="shift")
-        nc.vector.tensor_tensor(
-            shift[:].rearrange("p t (v j) -> p t v j", j=GROUP),
-            group_sum[:].unsqueeze(3).to_broadcast([P, TILES, Q // GROUP, GROUP]),
-            lam_rows[:].rearrange("p (v j) -> p v j", j=GROUP).unsqueeze(1).to_broadcast([P, TILES, Q // GROUP, GROUP]),
-            ALU.mult,
-        )
-        score = ps.tile([Q, TILES, P], F32, name="score", tag="bank3")
-        for n, src in enumerate((a0_sb, shift)):
-            for t in range(TILES):
-                nc.tensor.matmul(
-                    score[:, t, :],
-                    src[:, t, :],
-                    ident[:],
-                    is_transpose=True,
-                    start=(n == 0 and t == 0),
-                    stop=(n == 1 and t == TILES - 1),
-                )
-        score_row = score[:].rearrange("p t s -> p (t s)")
-
-        unused = sb.tile([Q, I], F32, name="unused")
-        neg_mean = sb.tile([Q, 1], F32, name="neg_mean")
-        nc.scalar.activation(unused[:], score_row, ACT.Identity, scale=mean_scale[:], accum_out=neg_mean[:])
-        z_sq = sb.tile([Q, I], F32, name="z_sq")
-        nc.scalar.activation(z_sq[:], score_row, ACT.Square, bias=neg_mean[:], scale=inv_width[:])
-        root = sb.tile([Q, I], F32, name="root")
-        nc.scalar.activation(root[:], z_sq[:], ACT.Abs_reciprocal_sqrt, bias=1.0)
-        part = sb.tile([Q, I], F32, name="part", tag="pick2", align_bytes=64)
-        part_sum = sb.tile([Q, 1], F32, name="part_sum")
-        nc.scalar.activation(part[:], root[:], ACT.Square, accum_out=part_sum[:])
-        def turn_and_quantise(rows, name, bank):
-            words = rows[:].bitcast(F32)
+        def turn(word_sets, name, bank, copy, tag):
             turned = ps.tile([P, 2, P], F32, name=f"{name}_turned", tag=bank)
             for u in range(2):
-                nc.tensor.transpose(turned[:, u, :], words[:, u : I // 2 : 2], ident[:])
-            grouped = sb.tile([P, P * PACK], BF16, name=f"{name}_grouped", align_bytes=64)
-            nc.scalar.copy(
-                grouped[:].bitcast(F32).rearrange("p (c u) -> p c u", u=2), turned[:].rearrange("p u c -> p c u")
-            )
-            codes = sb.tile([P, P], U32, name=f"{name}_codes", align_bytes=64)
+                nc.tensor.transpose(turned[:, u, :], word_sets[u], ident[:])
+            grouped = sb.tile([P, P * PACK], BF16, name=f"{name}_grouped", tag=tag, align_bytes=64)
+            copy(grouped[:].bitcast(F32).rearrange("p (c u) -> p c u", u=2), turned[:].rearrange("p u c -> p c u"))
+            return grouped
+
+        def quantise(grouped, name, tag):
+            codes = sb.tile([P, P], U32, name=f"{name}_codes", tag=tag, align_bytes=64)
             scales = sb.tile([P, P], U8, name=f"{name}_scales", align_bytes=64)
             nc.vector.quantize_mx(out=codes[:].bitcast(FP8X4), scales=scales[:], in_=grouped[:])
             return codes, scales
 
-        v_ops = []
-
-        def pick_values(j):
-            picked = sb.tile([P, I], BF16, name=f"picked{j}", tag=f"pick{j}", align_bytes=64)
+        def pick(j, tag):
+            picked = sb.tile([P, I], BF16, name=f"picked{j}", tag=tag, align_bytes=64)
             nc.vector.tensor_copy(picked[:], val_planes[j][:].indirect(offsets[:]))
-            v_ops.append(turn_and_quantise(picked, f"v{j}", f"bank{4 + j}"))
+            words = picked[:].bitcast(F32)
+            return [words[:, u : I // 2 : 2] for u in range(2)]
 
-        for j in range(2):
-            pick_values(j)
+        picked0 = pick(0, "sums1")
+        picked1 = pick(1, "sums0")
+        values = [quantise(turn(picked0, "v0", "bank5", nc.vector.tensor_copy, "big1"), "v0", "v0_codes")]
+        picked2 = pick(2, "big1")
 
-        inv_sum = sb.tile([Q, 1], F32, name="inv_sum", tag="big1")
+        inv_sum = sb.tile([Q, 1], F32, name="inv_sum", tag="big2", align_bytes=64)
         nc.vector.reciprocal(inv_sum[:], part_sum[:])
-        weight = sb.tile([Q, I], BF16, name="weight", align_bytes=64)
-        nc.vector.scalar_tensor_tensor(
-            weight[:].rearrange("q (s t) -> q s t", t=PACK),
-            part[:].rearrange("q (s t) -> q s t", t=PACK),
-            inv_sum[:],
-            factor_rows[:].rearrange("q t s -> q s t"),
-            ALU.mult,
-            ALU.mult,
-        )
+        pairs = []
+        for u in range(2):
+            weight = sb.tile([Q, HALF], BF16, name=f"weight{u}", align_bytes=64)
+            nc.vector.scalar_tensor_tensor(
+                weight[:].rearrange("q (s r) -> q s r", r=2),
+                part[:].rearrange("q (s t) -> q s t", t=PACK)[:, :, 2 * u : 2 * u + 2],
+                inv_sum[:],
+                factor_rows[:, 2 * u : 2 * u + 2, :].rearrange("q r s -> q s r"),
+                ALU.mult,
+                ALU.mult,
+            )
+            pairs.append(weight[:].bitcast(F32))
+        grouped1 = turn(picked1, "v1", "bank6", nc.scalar.copy, "root")
+        grouped2 = turn(picked2, "v2", "bank6", nc.scalar.copy, "v2_grouped")
+        grouped_w = turn(pairs, "w", "bank3", nc.scalar.copy, "w_grouped")
+        grouped3 = turn(pick(3, "part"), "v3", "bank4", nc.scalar.copy, "v3_grouped")
+        w_codes, w_scales = quantise(grouped_w, "w", "big3")
+        values.append(quantise(grouped1, "v1", "w_grouped"))
+        values.append(quantise(grouped2, "v2", "root"))
+        values.append(quantise(grouped3, "v3", "v2_grouped"))
 
-        w_codes, w_scales = turn_and_quantise(weight, "w", "bank0")
-
-        for j in range(2, PLANES):
-            pick_values(j)
-
-        for first, last, bank in ((0, PLANES - 1, "bank2"), (PLANES - 1, PLANES, "bank3")):
-            n = (last - first) * P
-            cols = slice(first * P, last * P)
-            acc = ps.tile([Q, n], F32, name=f"acc{first}", tag=bank)
+        spans = ((0, PLANES - 1), (PLANES - 1, PLANES))
+        accs = []
+        for n, (first, last) in enumerate(spans):
+            acc = ps.tile([Q, (last - first) * P], F32, name=f"acc{first}", tag=f"bank{1 + n}")
             for j in range(first, last):
                 nc.tensor.matmul_mx(
                     out=acc[:, (j - first) * P : (j - first + 1) * P],
                     lhsT=w_codes[:].bitcast(FP8X4),
                     lhsT_scale=w_scales[:],
-                    rhs=v_ops[j][0][:].bitcast(FP8X4),
-                    rhs_scale=v_ops[j][1][:],
+                    rhs=values[j][0][:].bitcast(FP8X4),
+                    rhs_scale=values[j][1][:],
                     start=True,
                     stop=True,
                 )
-            below = sb.tile([Q, n], F32, name=f"below{first}", tag=f"big{3 - first}")
-            nc.vector.scalar_tensor_tensor(below[:], acc[:], 0.1, floor_sb[:, cols], ALU.mult, ALU.add)
+            accs.append(acc)
+        for acc, (first, last) in zip(accs, spans):
+            n = (last - first) * P
+            below = sb.tile([Q, n], F32, name=f"below{first}", tag="v3_grouped" if first == 0 else "below", align_bytes=64)
+            nc.vector.scalar_tensor_tensor(below[:], acc[:], 0.1, floor_tiles[first][:], ALU.mult, ALU.add)
             above = sb.tile([Q, n], F32, name=f"above{first}")
-            nc.vector.scalar_tensor_tensor(above[:], floor_sb[:, cols], 0.1, acc[:], ALU.mult, ALU.add)
+            nc.vector.scalar_tensor_tensor(above[:], floor_tiles[first][:], 0.1, acc[:], ALU.mult, ALU.add)
             result = sb.tile([Q, n], F32, name=f"result{first}")
             nc.vector.tensor_tensor(result[:], below[:], above[:], ALU.max)
-            nc.sync.dma_start(out[:, cols], result[:])
+            nc.sync.dma_start(out[:, first * P : last * P], result[:])

@@ -25,6 +25,7 @@ PLANES = E // P
 
 HALF = I // 2
 HEAD = 512
+PLANE_BYTES = 4 * T
 
 
 def tile_attend_beyondgroup_typical_atleast_kernel(
@@ -33,13 +34,16 @@ def tile_attend_beyondgroup_typical_atleast_kernel(
     nc = tc.nc
     with ExitStack() as ctx:
         sb = ctx.enter_context(tc.tile_pool(name="sb", bufs=1))
+        placed = ctx.enter_context(tc.tile_pool(name="placed", bufs=1))
         ps = ctx.enter_context(tc.psum_pool(name="ps", bufs=1))
 
         offsets = sb.tile([P, I // 16], U16, name="offsets")
         nc.sync.dma_start(offsets[:], offs)
         q_raw = sb.tile([P, PACK, Q], F32, name="q_raw")
         nc.sync.dma_start(q_raw[:], query.rearrange("(p t) q -> p t q", t=PACK))
-        val_planes = [sb.tile([P, T], F32, name=f"val_plane{j}", tag=f"big{j}", align_bytes=64) for j in range(PLANES)]
+        val_planes = [
+            placed.tile([P, T], F32, name=f"val_plane{j}", offset=j * PLANE_BYTES, align_bytes=64) for j in range(PLANES)
+        ]
         nc.sync.dma_start(val_planes[0][:, :HEAD], vals[0:P, :HEAD])
 
         key_bytes = sb.tile([P, T], U8, name="key_bytes")
@@ -55,17 +59,17 @@ def tile_attend_beyondgroup_typical_atleast_kernel(
         )
         lam_col = sb.tile([Q, 1], F32, name="lam_col")
         width_col = sb.tile([Q, 1], F32, name="width_col")
-        factor4 = sb.tile([P, PACK], F32, name="factor4")
+        factor4 = sb.tile([P, PACK], F32, name="factor4", tag="factor4")
         with nc.allow_non_contiguous_dma(reason="one value a partition"):
             nc.sync.dma_start(lam_col[:], lam.rearrange("o q -> q o"))
             nc.sync.dma_start(val_planes[0][:, HEAD:], vals[0:P, HEAD:])
             nc.sync.dma_start(width_col[:], width)
         nc.sync.dma_start(val_planes[1][:], vals[P : 2 * P, :])
+        nc.sync.dma_start(val_planes[2][:], vals[2 * P : 3 * P, :])
         nc.sync.dma_start(factor4[:], slot_factor.rearrange("o (p t) -> p (o t)", t=PACK))
-        for j in range(2, PLANES):
-            nc.sync.dma_start(val_planes[j][:], vals[j * P : (j + 1) * P, :])
+        nc.sync.dma_start(val_planes[3][:], vals[3 * P : 4 * P, :])
         floor_tiles = {}
-        for first, last in ((0, PLANES - 1), (PLANES - 1, PLANES)):
+        for first, last in ((0, 2), (2, PLANES)):
             tile = sb.tile([Q, (last - first) * P], F32, name=f"floor{first}", tag=f"floor{first}", align_bytes=64)
             nc.sync.dma_start(tile[:], floors[:, first * P : last * P])
             floor_tiles[first] = tile
@@ -117,10 +121,13 @@ def tile_attend_beyondgroup_typical_atleast_kernel(
                 ALU.add,
             )
             group_sum.append(sums)
-        score = []
+        negated = []
         for h in range(2):
             neg_a0 = sb.tile([P, 2, Q], F32, name=f"neg_a0_{h}")
             nc.scalar.activation(neg_a0[:], a0[h][:], ACT.Copy, scale=-1.0)
+            negated.append(neg_a0)
+        score = []
+        for h in range(2):
             shift = sb.tile([P, 2, Q], F32, name=f"shift{h}")
             nc.vector.tensor_tensor(
                 shift[:].rearrange("p t (v j) -> p t v j", j=GROUP),
@@ -129,7 +136,7 @@ def tile_attend_beyondgroup_typical_atleast_kernel(
                 ALU.mult,
             )
             bank = ps.tile([Q, 2, P], F32, name=f"score{h}", tag=f"bank{3 + h}")
-            for n, src in enumerate((neg_a0, shift)):
+            for n, src in enumerate((negated[h], shift)):
                 for t in range(2):
                     nc.tensor.matmul(
                         bank[:, t, :], src[:, t, :], ident[:], is_transpose=True,
@@ -155,41 +162,45 @@ def tile_attend_beyondgroup_typical_atleast_kernel(
         for h in range(2):
             cols = slice(h * HALF, (h + 1) * HALF)
             nc.scalar.activation(root[:, cols], z_sq[:, cols], ACT.Abs_reciprocal_sqrt, bias=width_sq[:])
-        part = sb.tile([Q, I], F32, name="part", tag="part", align_bytes=64)
-        part_sum = sb.tile([Q, 1], F32, name="part_sum")
+        part = sb.tile([Q, I], F32, name="part")
+        part_sum = placed.tile([Q, 1], F32, name="part_sum", offset=PLANES * PLANE_BYTES, align_bytes=64)
         nc.scalar.activation(part[:], root[:], ACT.Square, accum_out=part_sum[:])
 
         factor_rows = ps.tile([P, PACK, P], F32, name="factor_rows", tag="bank0")
         for t in range(PACK):
             nc.tensor.transpose(factor_rows[:, t, :], factor4[:, t : t + 1].to_broadcast([P, P]), ident[:])
 
-        def turn(word_sets, name, bank, copy, tag):
+        def turn(word_sets, name, bank, grouped):
             turned = ps.tile([P, 2, P], F32, name=f"{name}_turned", tag=bank)
             for u in range(2):
                 nc.tensor.transpose(turned[:, u, :], word_sets[u], ident[:])
-            grouped = sb.tile([P, P * PACK], BF16, name=f"{name}_grouped", tag=tag, align_bytes=64)
-            copy(grouped[:].bitcast(F32).rearrange("p (c u) -> p c u", u=2), turned[:].rearrange("p u c -> p c u"))
-            return grouped
+            nc.scalar.copy(
+                grouped.bitcast(F32).rearrange("p (c u) -> p c u", u=2), turned[:].rearrange("p u c -> p c u")
+            )
 
-        def quantise(grouped, name, tag):
-            codes = sb.tile([P, P], U32, name=f"{name}_codes", tag=tag, align_bytes=64)
-            scales = sb.tile([P, P], U8, name=f"{name}_scales", align_bytes=64)
-            nc.vector.quantize_mx(out=codes[:].bitcast(FP8X4), scales=scales[:], in_=grouped[:])
+        def quantise(grouped, name, offset):
+            columns = grouped.shape[1] // PACK
+            codes = placed.tile([P, columns], U32, name=f"{name}_codes", offset=offset, align_bytes=64)
+            scales = sb.tile([P, columns], U8, name=f"{name}_scales", align_bytes=64)
+            nc.vector.quantize_mx(out=codes[:].bitcast(FP8X4), scales=scales[:], in_=grouped)
             return codes, scales
 
-        def pick(j, tag):
-            picked = sb.tile([P, I], BF16, name=f"picked{j}", tag=tag, align_bytes=64)
+        def pick(j, tag, pool=sb, **place):
+            picked = pool.tile([P, I], BF16, name=f"picked{j}", tag=tag, align_bytes=64, **place)
             nc.vector.tensor_copy(picked[:], val_planes[j][:].indirect(offsets[:]))
             words = picked[:].bitcast(F32)
             return [words[:, u : I // 2 : 2] for u in range(2)]
 
-        picked0 = pick(0, "sums1")
-        picked1 = pick(1, "sums0")
-        values = [quantise(turn(picked0, "v0", "bank5", nc.vector.tensor_copy, "big1"), "v0", "v0_codes")]
-        picked2 = pick(2, "big1")
+        picked = [pick(0, "sums1"), pick(1, "sums0")]
+        grouped01 = sb.tile([P, 2 * I], BF16, name="grouped01", tag="root", align_bytes=64)
+        for j in range(2):
+            turn(picked[j], f"v{j}", f"bank{5 + j}", grouped01[:, j * I : (j + 1) * I])
 
-        inv_sum = sb.tile([Q, 1], F32, name="inv_sum", tag="big2", align_bytes=64)
+        picked2 = pick(2, "picked2")
+
+        inv_sum = sb.tile([Q, 1], F32, name="inv_sum", tag="factor4")
         nc.vector.reciprocal(inv_sum[:], part_sum[:])
+        values01 = quantise(grouped01[:], "v01", PLANES * PLANE_BYTES)
         pairs = []
         for u in range(2):
             weight = sb.tile([Q, HALF], BF16, name=f"weight{u}", align_bytes=64)
@@ -202,36 +213,54 @@ def tile_attend_beyondgroup_typical_atleast_kernel(
                 ALU.mult,
             )
             pairs.append(weight[:].bitcast(F32))
-        grouped1 = turn(picked1, "v1", "bank6", nc.scalar.copy, "root")
-        grouped2 = turn(picked2, "v2", "bank6", nc.scalar.copy, "v2_grouped")
-        grouped_w = turn(pairs, "w", "bank3", nc.scalar.copy, "w_grouped")
-        grouped3 = turn(pick(3, "part"), "v3", "bank4", nc.scalar.copy, "v3_grouped")
-        w_codes, w_scales = quantise(grouped_w, "w", "big3")
-        values.append(quantise(grouped1, "v1", "w_grouped"))
-        values.append(quantise(grouped2, "v2", "root"))
-        values.append(quantise(grouped3, "v3", "v2_grouped"))
+        grouped_w = sb.tile([P, I], BF16, name="grouped_w", align_bytes=64)
+        turn(pairs, "w", "bank3", grouped_w[:])
 
-        spans = ((0, PLANES - 1), (PLANES - 1, PLANES))
-        accs = []
-        for n, (first, last) in enumerate(spans):
-            acc = ps.tile([Q, (last - first) * P], F32, name=f"acc{first}", tag=f"bank{1 + n}")
-            for j in range(first, last):
-                nc.tensor.matmul_mx(
-                    out=acc[:, (j - first) * P : (j - first + 1) * P],
-                    lhsT=w_codes[:].bitcast(FP8X4),
-                    lhsT_scale=w_scales[:],
-                    rhs=values[j][0][:].bitcast(FP8X4),
-                    rhs_scale=values[j][1][:],
-                    start=True,
-                    stop=True,
-                )
-            accs.append(acc)
-        for acc, (first, last) in zip(accs, spans):
-            n = (last - first) * P
-            below = sb.tile([Q, n], F32, name=f"below{first}", tag="v3_grouped" if first == 0 else "below", align_bytes=64)
+        grouped2 = sb.tile([P, I], BF16, name="grouped2", align_bytes=64)
+        turn(picked2, "v2", "bank3", grouped2[:])
+        grouped3 = sb.tile([P, I], BF16, name="grouped3", align_bytes=64)
+        turn(pick(3, "picked3", placed, offset=2 * PLANE_BYTES), "v3", "bank4", grouped3[:])
+        weights = quantise(grouped_w[:], "w", 3 * PLANE_BYTES)
+        values2 = quantise(grouped2[:], "v2", 3 * PLANE_BYTES + 512)
+
+        def multiply(acc, values):
+            nc.tensor.matmul_mx(
+                out=acc,
+                lhsT=weights[0][:].bitcast(FP8X4),
+                lhsT_scale=weights[1][:],
+                rhs=values[0][:].bitcast(FP8X4),
+                rhs_scale=values[1][:],
+                start=True,
+                stop=True,
+            )
+
+        def floor_side(acc, first):
+            below = sb.tile([Q, 2 * P], F32, name=f"below{first}")
             nc.vector.scalar_tensor_tensor(below[:], acc[:], 0.1, floor_tiles[first][:], ALU.mult, ALU.add)
-            above = sb.tile([Q, n], F32, name=f"above{first}")
+            return below
+
+        def sum_side(acc, first):
+            above = sb.tile([Q, 2 * P], F32, name=f"above{first}")
             nc.vector.scalar_tensor_tensor(above[:], floor_tiles[first][:], 0.1, acc[:], ALU.mult, ALU.add)
-            result = sb.tile([Q, n], F32, name=f"result{first}")
+            return above
+
+        def finish(first, below, above):
+            result = sb.tile([Q, 2 * P], F32, name=f"result{first}")
             nc.vector.tensor_tensor(result[:], below[:], above[:], ALU.max)
-            nc.sync.dma_start(out[:, first * P : last * P], result[:])
+            nc.sync.dma_start(out[:, first * P : (first + 2) * P], result[:])
+
+        values3 = quantise(grouped3[:], "v3", 3 * PLANE_BYTES + 1024)
+        acc01 = ps.tile([Q, 2 * P], F32, name="acc01", tag="bank1")
+        multiply(acc01[:], values01)
+        acc23 = ps.tile([Q, 2 * P], F32, name="acc23", tag="bank2")
+        multiply(acc23[:, :P], values2)
+        multiply(acc23[:, P:], values3)
+        excess = sb.tile([Q, 2 * P], F32, name="excess")
+        nc.vector.tensor_tensor(excess[:], acc01[:], floor_tiles[0][:], ALU.subtract)
+        below01 = floor_side(acc01, 0)
+        lift = sb.tile([Q, 2 * P], F32, name="lift")
+        nc.scalar.activation(lift[:], excess[:], ACT.Relu, scale=0.9)
+        result01 = sb.tile([Q, 2 * P], F32, name="result01")
+        nc.gpsimd.tensor_tensor(result01[:], below01[:], lift[:], ALU.add)
+        nc.sync.dma_start(out[:, : 2 * P], result01[:])
+        finish(2, floor_side(acc23, 2), sum_side(acc23, 2))

@@ -19,13 +19,15 @@ ACT = mybir.ActivationFunctionType
 P = 128
 PACK = 4
 GROUP = 8
-TILES = I // P
 PLANES = E // P
-
-
 HALF = I // 2
+LIST_ROWS = 16
 HEAD = 512
+PAIR = 2 * P
 PLANE_BYTES = 4 * T
+CODES_BYTES = 4 * P
+LAST_GROUPED = PLANES * PLANE_BYTES + 4 * CODES_BYTES
+SMALL_SHARE = 0.1
 
 
 def tile_attend_beyondgroup_typical_atleast_kernel(
@@ -37,7 +39,7 @@ def tile_attend_beyondgroup_typical_atleast_kernel(
         placed = ctx.enter_context(tc.tile_pool(name="placed", bufs=1))
         ps = ctx.enter_context(tc.psum_pool(name="ps", bufs=1))
 
-        offsets = sb.tile([P, I // 16], U16, name="offsets")
+        offsets = sb.tile([P, I // LIST_ROWS], U16, name="offsets")
         nc.sync.dma_start(offsets[:], offs)
         q_raw = sb.tile([P, PACK, Q], F32, name="q_raw")
         nc.sync.dma_start(q_raw[:], query.rearrange("(p t) q -> p t q", t=PACK))
@@ -54,13 +56,11 @@ def tile_attend_beyondgroup_typical_atleast_kernel(
                 keys_scales[0, 4 * quad : 4 * quad + 4, :].bitcast(I32),
             )
         key_words = sb.tile([P, T], U32, name="key_words")
-        nc.sync.dma_start(
-            key_words[:].bitcast(I32), keys_words[0].rearrange("p n t -> p (n t)").bitcast(I32)
-        )
+        nc.sync.dma_start(key_words[:].bitcast(I32), keys_words[0].rearrange("p n t -> p (n t)").bitcast(I32))
         lam_col = sb.tile([Q, 1], F32, name="lam_col")
         width_col = sb.tile([Q, 1], F32, name="width_col")
         factor4 = sb.tile([P, PACK], F32, name="factor4", tag="factor4")
-        with nc.allow_non_contiguous_dma(reason="one value a partition"):
+        with nc.allow_non_contiguous_dma(reason="lam and width are loaded one value a partition"):
             nc.sync.dma_start(lam_col[:], lam.rearrange("o q -> q o"))
             nc.sync.dma_start(val_planes[0][:, HEAD:], vals[0:P, HEAD:])
             nc.sync.dma_start(width_col[:], width)
@@ -68,11 +68,11 @@ def tile_attend_beyondgroup_typical_atleast_kernel(
         nc.sync.dma_start(val_planes[2][:], vals[2 * P : 3 * P, :])
         nc.sync.dma_start(factor4[:], slot_factor.rearrange("o (p t) -> p (o t)", t=PACK))
         nc.sync.dma_start(val_planes[3][:], vals[3 * P : 4 * P, :])
-        floor_tiles = {}
-        for first, last in ((0, 2), (2, PLANES)):
-            tile = sb.tile([Q, (last - first) * P], F32, name=f"floor{first}", tag=f"floor{first}", align_bytes=64)
-            nc.sync.dma_start(tile[:], floors[:, first * P : last * P])
-            floor_tiles[first] = tile
+        floor_pairs = []
+        for n in range(E // PAIR):
+            floor_pair = sb.tile([Q, PAIR], F32, name=f"floor{n}", align_bytes=64)
+            nc.sync.dma_start(floor_pair[:], floors[:, n * PAIR : (n + 1) * PAIR])
+            floor_pairs.append(floor_pair)
 
         ident = sb.tile([P, P], F32, name="ident")
         make_identity(nc, ident[:])
@@ -80,7 +80,6 @@ def tile_attend_beyondgroup_typical_atleast_kernel(
         nc.vector.memset(one[:], 1.0)
         warm = sb.tile([P, 1], F32, name="warm")
         nc.scalar.activation(warm[:], one[:], ACT.Abs_reciprocal_sqrt)
-
 
         q_grouped = sb.tile([P, Q, PACK], BF16, name="q_grouped", align_bytes=64)
         nc.scalar.copy(q_grouped[:], q_raw[:].rearrange("p t q -> p q t"))
@@ -91,22 +90,24 @@ def tile_attend_beyondgroup_typical_atleast_kernel(
         nc.vector.quantize_mx(
             out=q_codes[:].bitcast(FP8X4), scales=q_scales[:], in_=q_grouped[:].rearrange("p q t -> p (q t)")
         )
+
         a0 = []
         for h in range(2):
+            list_cols = slice(h * HALF // LIST_ROWS, (h + 1) * HALF // LIST_ROWS)
             k_codes = sb.tile([P, HALF], U32, name=f"k_codes{h}", align_bytes=64)
-            nc.vector.tensor_copy(k_codes[:], key_words[:].indirect(offsets[:, h * 16 : (h + 1) * 16]))
-            bank = ps.tile([P, 2, Q], F32, name=f"a0_{h}", tag=f"bank{1 + h}")
-            for t in range(2):
+            nc.vector.tensor_copy(k_codes[:], key_words[:].indirect(offsets[:, list_cols]))
+            products = ps.tile([P, 2, Q], F32, name=f"a0_{h}", tag=f"bank{1 + h}")
+            for c in range(2):
                 nc.tensor.matmul_mx(
-                    out=bank[:, t, :],
-                    lhsT=k_codes[:, t * P : (t + 1) * P].bitcast(FP8X4),
-                    lhsT_scale=k_scales[:, h * HALF + t * P : h * HALF + (t + 1) * P],
+                    out=products[:, c, :],
+                    lhsT=k_codes[:, c * P : (c + 1) * P].bitcast(FP8X4),
+                    lhsT_scale=k_scales[:, h * HALF + c * P : h * HALF + (c + 1) * P],
                     rhs=q_codes[:].bitcast(FP8X4),
                     rhs_scale=q_scales[:],
                     start=True,
                     stop=True,
                 )
-            a0.append(bank)
+            a0.append(products)
 
         lam_rows = ps.tile([P, Q], F32, name="lam_rows", tag="bank0")
         nc.tensor.transpose(lam_rows[:], lam_col[:].to_broadcast([P, P]), ident[:])
@@ -115,53 +116,58 @@ def tile_attend_beyondgroup_typical_atleast_kernel(
         for h in range(2):
             sums = sb.tile([P, 2, Q // GROUP], F32, name=f"group_sum{h}", tag=f"sums{h}", align_bytes=64)
             nc.vector.tensor_reduce(
-                sums[:].rearrange("p t v -> p (t v)"),
-                a0[h][:].rearrange("p t (v j) -> p (t v) j", j=GROUP),
+                sums[:].rearrange("p c v -> p (c v)"),
+                a0[h][:].rearrange("p c (v j) -> p (c v) j", j=GROUP),
                 mybir.AxisListType.X,
                 ALU.add,
             )
             group_sum.append(sums)
-        negated = []
+        neg_a0 = []
         for h in range(2):
-            neg_a0 = sb.tile([P, 2, Q], F32, name=f"neg_a0_{h}")
-            nc.scalar.activation(neg_a0[:], a0[h][:], ACT.Copy, scale=-1.0)
-            negated.append(neg_a0)
-        score = []
+            negated = sb.tile([P, 2, Q], F32, name=f"neg_a0_{h}")
+            nc.scalar.activation(negated[:], a0[h][:], ACT.Copy, scale=-1.0)
+            neg_a0.append(negated)
+        neg_score = []
+        by_group = [P, 2, Q // GROUP, GROUP]
         for h in range(2):
             shift = sb.tile([P, 2, Q], F32, name=f"shift{h}")
             nc.vector.tensor_tensor(
-                shift[:].rearrange("p t (v j) -> p t v j", j=GROUP),
-                group_sum[h][:].unsqueeze(3).to_broadcast([P, 2, Q // GROUP, GROUP]),
-                lam_rows[:].rearrange("p (v j) -> p v j", j=GROUP).unsqueeze(1).to_broadcast([P, 2, Q // GROUP, GROUP]),
+                shift[:].rearrange("p c (v j) -> p c v j", j=GROUP),
+                group_sum[h][:].unsqueeze(3).to_broadcast(by_group),
+                lam_rows[:].rearrange("p (v j) -> p v j", j=GROUP).unsqueeze(1).to_broadcast(by_group),
                 ALU.mult,
             )
-            bank = ps.tile([Q, 2, P], F32, name=f"score{h}", tag=f"bank{3 + h}")
-            for n, src in enumerate((negated[h], shift)):
-                for t in range(2):
+            turned_score = ps.tile([Q, 2, P], F32, name=f"score{h}", tag=f"bank{3 + h}")
+            for n, term in enumerate((neg_a0[h], shift)):
+                for c in range(2):
                     nc.tensor.matmul(
-                        bank[:, t, :], src[:, t, :], ident[:], is_transpose=True,
-                        start=(n == 0 and t == 0), stop=(n == 1 and t == 1),
+                        turned_score[:, c, :],
+                        term[:, c, :],
+                        ident[:],
+                        is_transpose=True,
+                        start=(n == 0 and c == 0),
+                        stop=(n == 1 and c == 1),
                     )
-            score.append(bank[:].rearrange("p t s -> p (t s)"))
+            neg_score.append(turned_score[:].rearrange("p c s -> p (c s)"))
 
         width_sq = sb.tile([Q, 1], F32, name="width_sq")
         nc.gpsimd.tensor_tensor(width_sq[:], width_col[:], width_col[:], ALU.mult)
-        unused = sb.tile([Q, I], F32, name="unused")
+        summands = sb.tile([Q, I], F32, name="summands")
         first_share = sb.tile([Q, 1], F32, name="first_share")
-        nc.scalar.activation(unused[:, :HALF], score[0], ACT.Identity, scale=-1.0 / (I * HALF), accum_out=first_share[:])
-        neg_mean = sb.tile([Q, 1], F32, name="neg_mean")
         nc.scalar.activation(
-            unused[:, HALF:], score[1], ACT.Identity, bias=first_share[:], scale=-1.0 / I, accum_out=neg_mean[:]
+            summands[:, :HALF], neg_score[0], ACT.Identity, scale=-1.0 / (I * HALF), accum_out=first_share[:]
         )
-        z_sq = sb.tile([Q, I], F32, name="z_sq")
+        mean = sb.tile([Q, 1], F32, name="mean")
+        nc.scalar.activation(
+            summands[:, HALF:], neg_score[1], ACT.Identity, bias=first_share[:], scale=-1.0 / I, accum_out=mean[:]
+        )
+        x_sq = sb.tile([Q, I], F32, name="x_sq")
         for h in range(2):
-            nc.scalar.activation(
-                z_sq[:, h * HALF : (h + 1) * HALF], score[h], ACT.Square, bias=neg_mean[:]
-            )
+            nc.scalar.activation(x_sq[:, h * HALF : (h + 1) * HALF], neg_score[h], ACT.Square, bias=mean[:])
         root = sb.tile([Q, I], F32, name="root", tag="root", align_bytes=64)
         for h in range(2):
             cols = slice(h * HALF, (h + 1) * HALF)
-            nc.scalar.activation(root[:, cols], z_sq[:, cols], ACT.Abs_reciprocal_sqrt, bias=width_sq[:])
+            nc.scalar.activation(root[:, cols], x_sq[:, cols], ACT.Abs_reciprocal_sqrt, bias=width_sq[:])
         part = sb.tile([Q, I], F32, name="part")
         part_sum = placed.tile([Q, 1], F32, name="part_sum", offset=PLANES * PLANE_BYTES, align_bytes=64)
         nc.scalar.activation(part[:], root[:], ACT.Square, accum_out=part_sum[:])
@@ -185,23 +191,22 @@ def tile_attend_beyondgroup_typical_atleast_kernel(
             nc.vector.quantize_mx(out=codes[:].bitcast(FP8X4), scales=scales[:], in_=grouped)
             return codes, scales
 
-        def pick(j, tag, pool=sb, **place):
-            picked = pool.tile([P, I], BF16, name=f"picked{j}", tag=tag, align_bytes=64, **place)
+        def pick(j, pool, **place):
+            picked = pool.tile([P, I], BF16, name=f"picked{j}", align_bytes=64, **place)
             nc.vector.tensor_copy(picked[:], val_planes[j][:].indirect(offsets[:]))
             words = picked[:].bitcast(F32)
             return [words[:, u : I // 2 : 2] for u in range(2)]
 
-        picked = [pick(0, "sums1"), pick(1, "sums0")]
+        picked01 = [pick(0, sb, tag="sums1"), pick(1, sb, tag="sums0")]
         grouped01 = sb.tile([P, 2 * I], BF16, name="grouped01", tag="root", align_bytes=64)
         for j in range(2):
-            turn(picked[j], f"v{j}", f"bank{5 + j}", grouped01[:, j * I : (j + 1) * I])
-
-        picked2 = pick(2, "picked2")
+            turn(picked01[j], f"v{j}", f"bank{5 + j}", grouped01[:, j * I : (j + 1) * I])
+        picked2 = pick(2, sb)
 
         inv_sum = sb.tile([Q, 1], F32, name="inv_sum", tag="factor4")
         nc.vector.reciprocal(inv_sum[:], part_sum[:])
         values01 = quantise(grouped01[:], "v01", PLANES * PLANE_BYTES)
-        pairs = []
+        weight_words = []
         for u in range(2):
             weight = sb.tile([Q, HALF], BF16, name=f"weight{u}", align_bytes=64)
             nc.vector.scalar_tensor_tensor(
@@ -212,16 +217,17 @@ def tile_attend_beyondgroup_typical_atleast_kernel(
                 ALU.mult,
                 ALU.mult,
             )
-            pairs.append(weight[:].bitcast(F32))
+            weight_words.append(weight[:].bitcast(F32))
         grouped_w = sb.tile([P, I], BF16, name="grouped_w", align_bytes=64)
-        turn(pairs, "w", "bank3", grouped_w[:])
+        turn(weight_words, "w", "bank3", grouped_w[:])
 
         grouped2 = sb.tile([P, I], BF16, name="grouped2", align_bytes=64)
         turn(picked2, "v2", "bank3", grouped2[:])
-        grouped3 = sb.tile([P, I], BF16, name="grouped3", align_bytes=64)
-        turn(pick(3, "picked3", placed, offset=2 * PLANE_BYTES), "v3", "bank4", grouped3[:])
+        grouped3 = placed.tile([P, I], BF16, name="grouped3", offset=LAST_GROUPED, align_bytes=64)
+        turn(pick(3, placed, offset=2 * PLANE_BYTES), "v3", "bank4", grouped3[:])
         weights = quantise(grouped_w[:], "w", 3 * PLANE_BYTES)
-        values2 = quantise(grouped2[:], "v2", 3 * PLANE_BYTES + 512)
+        values2 = quantise(grouped2[:], "v2", 3 * PLANE_BYTES + CODES_BYTES)
+        values3 = quantise(grouped3[:], "v3", 3 * PLANE_BYTES + 2 * CODES_BYTES)
 
         def multiply(acc, values):
             nc.tensor.matmul_mx(
@@ -234,33 +240,31 @@ def tile_attend_beyondgroup_typical_atleast_kernel(
                 stop=True,
             )
 
-        def floor_side(acc, first):
-            below = sb.tile([Q, 2 * P], F32, name=f"below{first}")
-            nc.vector.scalar_tensor_tensor(below[:], acc[:], 0.1, floor_tiles[first][:], ALU.mult, ALU.add)
-            return below
+        o01 = ps.tile([Q, PAIR], F32, name="o01", tag="bank1")
+        multiply(o01[:], values01)
+        o23 = []
+        for values, bank in ((values2, "bank2"), (values3, "bank5")):
+            o_plane = ps.tile([Q, P], F32, name=f"o_{bank}", tag=bank)
+            multiply(o_plane[:], values)
+            o23.append(o_plane)
 
-        def sum_side(acc, first):
-            above = sb.tile([Q, 2 * P], F32, name=f"above{first}")
-            nc.vector.scalar_tensor_tensor(above[:], floor_tiles[first][:], 0.1, acc[:], ALU.mult, ALU.add)
-            return above
-
-        def finish(first, below, above):
-            result = sb.tile([Q, 2 * P], F32, name=f"result{first}")
-            nc.vector.tensor_tensor(result[:], below[:], above[:], ALU.max)
-            nc.sync.dma_start(out[:, first * P : (first + 2) * P], result[:])
-
-        values3 = quantise(grouped3[:], "v3", 3 * PLANE_BYTES + 1024)
-        acc01 = ps.tile([Q, 2 * P], F32, name="acc01", tag="bank1")
-        multiply(acc01[:], values01)
-        acc23 = ps.tile([Q, 2 * P], F32, name="acc23", tag="bank2")
-        multiply(acc23[:, :P], values2)
-        multiply(acc23[:, P:], values3)
-        excess = sb.tile([Q, 2 * P], F32, name="excess")
-        nc.vector.tensor_tensor(excess[:], acc01[:], floor_tiles[0][:], ALU.subtract)
-        below01 = floor_side(acc01, 0)
-        lift = sb.tile([Q, 2 * P], F32, name="lift")
+        excess = sb.tile([Q, PAIR], F32, name="excess")
+        nc.vector.tensor_tensor(excess[:], o01[:], floor_pairs[0][:], ALU.subtract)
+        base = sb.tile([Q, PAIR], F32, name="base")
+        nc.vector.scalar_tensor_tensor(base[:], o01[:], SMALL_SHARE, floor_pairs[0][:], ALU.mult, ALU.add)
+        lift = sb.tile([Q, PAIR], F32, name="lift")
         nc.scalar.activation(lift[:], excess[:], ACT.Relu, scale=0.9)
-        result01 = sb.tile([Q, 2 * P], F32, name="result01")
-        nc.gpsimd.tensor_tensor(result01[:], below01[:], lift[:], ALU.add)
-        nc.sync.dma_start(out[:, : 2 * P], result01[:])
-        finish(2, floor_side(acc23, 2), sum_side(acc23, 2))
+        result01 = sb.tile([Q, PAIR], F32, name="result01")
+        nc.gpsimd.tensor_tensor(result01[:], base[:], lift[:], ALU.add)
+        nc.sync.dma_start(out[:, :PAIR], result01[:])
+
+        floor_larger = placed.tile([Q, PAIR], F32, name="floor_larger", offset=LAST_GROUPED - I, align_bytes=64)
+        o_larger = placed.tile([Q, PAIR], F32, name="o_larger", offset=LAST_GROUPED + I, align_bytes=64)
+        for n, o_plane in enumerate(o23):
+            cols = slice(n * P, (n + 1) * P)
+            floor_plane = floor_pairs[1][:, cols]
+            nc.vector.scalar_tensor_tensor(floor_larger[:, cols], o_plane[:], SMALL_SHARE, floor_plane, ALU.mult, ALU.add)
+            nc.vector.scalar_tensor_tensor(o_larger[:, cols], floor_plane, SMALL_SHARE, o_plane[:], ALU.mult, ALU.add)
+        result23 = sb.tile([Q, PAIR], F32, name="result23")
+        nc.vector.tensor_tensor(result23[:], floor_larger[:], o_larger[:], ALU.max)
+        nc.sync.dma_start(out[:, PAIR:], result23[:])

from contextlib import ExitStack

import concourse.mybir as mybir
from concourse.masks import make_identity

D, T, I, Q, E = 512, 2048, 512, 128, 512
FLOPS = 2 * I * D * Q + 2 * Q * I * E

F32 = mybir.dt.float32
BF16 = mybir.dt.bfloat16
I32 = mybir.dt.int32
U32 = mybir.dt.uint32
U16 = mybir.dt.uint16
U8 = mybir.dt.uint8
FP8X4 = mybir.dt.float8_e4m3fn_x4
ALU = mybir.AluOpType
ACT = mybir.ActivationFunctionType

P = 128
PACK = 4
GROUP = 8
PLANES = E // P
HALF = I // 2
LIST_ROWS = 16
HEAD = 512
PAIR = 2 * P
PLANE_BYTES = 4 * T
CODES_BYTES = 4 * P
LAST_GROUPED = PLANES * PLANE_BYTES + 4 * CODES_BYTES
SMALL_SHARE = 0.1


def tile_attend_beyondgroup_typical_atleast_kernel(
    tc, query, keys_words, keys_scales, lam, width, slot_factor, vals, floors, offs, out
):
    nc = tc.nc
    with ExitStack() as ctx:
        sb = ctx.enter_context(tc.tile_pool(name="sb", bufs=1))
        placed = ctx.enter_context(tc.tile_pool(name="placed", bufs=1))
        ps = ctx.enter_context(tc.psum_pool(name="ps", bufs=1))

        offsets = sb.tile([P, I // LIST_ROWS], U16, name="offsets")
        nc.sync.dma_start(offsets[:], offs)
        q_raw = sb.tile([P, PACK, Q], F32, name="q_raw")
        nc.sync.dma_start(q_raw[:], query.rearrange("(p t) q -> p t q", t=PACK))
        val_planes = [
            placed.tile([P, T], F32, name=f"val_plane{j}", offset=j * PLANE_BYTES, align_bytes=64) for j in range(PLANES)
        ]
        nc.sync.dma_start(val_planes[0][:, :HEAD], vals[0:P, :HEAD])

        key_bytes = sb.tile([P, T], U8, name="key_bytes")
        nc.vector.memset(key_bytes[:].bitcast(I32), 0)
        for quad in range(4):
            nc.sync.dma_start(
                key_bytes[32 * quad : 32 * quad + 4, :].bitcast(I32),
                keys_scales[0, 4 * quad : 4 * quad + 4, :].bitcast(I32),
            )
        key_words = sb.tile([P, T], U32, name="key_words")
        nc.sync.dma_start(key_words[:].bitcast(I32), keys_words[0].rearrange("p n t -> p (n t)").bitcast(I32))
        lam_col = sb.tile([Q, 1], F32, name="lam_col")
        width_col = sb.tile([Q, 1], F32, name="width_col")
        factor4 = sb.tile([P, PACK], F32, name="factor4", tag="factor4")
        with nc.allow_non_contiguous_dma(reason="lam and width are loaded one value a partition"):
            nc.sync.dma_start(lam_col[:], lam.rearrange("o q -> q o"))
            nc.sync.dma_start(val_planes[0][:, HEAD:], vals[0:P, HEAD:])
            nc.sync.dma_start(width_col[:], width)
        nc.sync.dma_start(val_planes[1][:], vals[P : 2 * P, :])
        nc.sync.dma_start(val_planes[2][:], vals[2 * P : 3 * P, :])
        nc.sync.dma_start(factor4[:], slot_factor.rearrange("o (p t) -> p (o t)", t=PACK))
        nc.sync.dma_start(val_planes[3][:], vals[3 * P : 4 * P, :])
        floor_pairs = []
        for n in range(E // PAIR):
            floor_pair = sb.tile([Q, PAIR], F32, name=f"floor{n}", align_bytes=64)
            nc.sync.dma_start(floor_pair[:], floors[:, n * PAIR : (n + 1) * PAIR])
            floor_pairs.append(floor_pair)

        ident = sb.tile([P, P], F32, name="ident")
        make_identity(nc, ident[:])
        one = sb.tile([P, 1], F32, name="one")
        nc.vector.memset(one[:], 1.0)
        warm = sb.tile([P, 1], F32, name="warm")
        nc.scalar.activation(warm[:], one[:], ACT.Abs_reciprocal_sqrt)

        q_grouped = sb.tile([P, Q, PACK], BF16, name="q_grouped", align_bytes=64)
        nc.scalar.copy(q_grouped[:], q_raw[:].rearrange("p t q -> p q t"))
        k_scales = sb.tile([P, I], U8, name="k_scales", align_bytes=64)
        nc.vector.tensor_copy(k_scales[:], key_bytes[:].indirect(offsets[:]))
        q_codes = sb.tile([P, Q], U32, name="q_codes", align_bytes=64)
        q_scales = sb.tile([P, Q], U8, name="q_scales", align_bytes=64)
        nc.vector.quantize_mx(
            out=q_codes[:].bitcast(FP8X4), scales=q_scales[:], in_=q_grouped[:].rearrange("p q t -> p (q t)")
        )

        a0 = []
        for h in range(2):
            list_cols = slice(h * HALF // LIST_ROWS, (h + 1) * HALF // LIST_ROWS)
            k_codes = sb.tile([P, HALF], U32, name=f"k_codes{h}", align_bytes=64)
            nc.vector.tensor_copy(k_codes[:], key_words[:].indirect(offsets[:, list_cols]))
            products = ps.tile([P, 2, Q], F32, name=f"a0_{h}", tag=f"bank{1 + h}")
            for c in range(2):
                nc.tensor.matmul_mx(
                    out=products[:, c, :],
                    lhsT=k_codes[:, c * P : (c + 1) * P].bitcast(FP8X4),
                    lhsT_scale=k_scales[:, h * HALF + c * P : h * HALF + (c + 1) * P],
                    rhs=q_codes[:].bitcast(FP8X4),
                    rhs_scale=q_scales[:],
                    start=True,
                    stop=True,
                )
            a0.append(products)

        lam_rows = ps.tile([P, Q], F32, name="lam_rows", tag="bank0")
        nc.tensor.transpose(lam_rows[:], lam_col[:].to_broadcast([P, P]), ident[:])

        group_sum = []
        for h in range(2):
            sums = sb.tile([P, 2, Q // GROUP], F32, name=f"group_sum{h}", tag=f"sums{h}", align_bytes=64)
            nc.vector.tensor_reduce(
                sums[:].rearrange("p c v -> p (c v)"),
                a0[h][:].rearrange("p c (v j) -> p (c v) j", j=GROUP),
                mybir.AxisListType.X,
                ALU.add,
            )
            group_sum.append(sums)
        neg_a0 = []
        for h in range(2):
            negated = sb.tile([P, 2, Q], F32, name=f"neg_a0_{h}")
            nc.scalar.activation(negated[:], a0[h][:], ACT.Copy, scale=-1.0)
            neg_a0.append(negated)
        neg_score = []
        by_group = [P, 2, Q // GROUP, GROUP]
        for h in range(2):
            shift = sb.tile([P, 2, Q], F32, name=f"shift{h}")
            nc.vector.tensor_tensor(
                shift[:].rearrange("p c (v j) -> p c v j", j=GROUP),
                group_sum[h][:].unsqueeze(3).to_broadcast(by_group),
                lam_rows[:].rearrange("p (v j) -> p v j", j=GROUP).unsqueeze(1).to_broadcast(by_group),
                ALU.mult,
            )
            turned_score = ps.tile([Q, 2, P], F32, name=f"score{h}", tag=f"bank{3 + h}")
            for n, term in enumerate((neg_a0[h], shift)):
                for c in range(2):
                    nc.tensor.matmul(
                        turned_score[:, c, :],
                        term[:, c, :],
                        ident[:],
                        is_transpose=True,
                        start=(n == 0 and c == 0),
                        stop=(n == 1 and c == 1),
                    )
            neg_score.append(turned_score[:].rearrange("p c s -> p (c s)"))

        width_sq = sb.tile([Q, 1], F32, name="width_sq")
        nc.gpsimd.tensor_tensor(width_sq[:], width_col[:], width_col[:], ALU.mult)
        summands = sb.tile([Q, I], F32, name="summands")
        first_share = sb.tile([Q, 1], F32, name="first_share")
        nc.scalar.activation(
            summands[:, :HALF], neg_score[0], ACT.Identity, scale=-1.0 / (I * HALF), accum_out=first_share[:]
        )
        mean = sb.tile([Q, 1], F32, name="mean")
        nc.scalar.activation(
            summands[:, HALF:], neg_score[1], ACT.Identity, bias=first_share[:], scale=-1.0 / I, accum_out=mean[:]
        )
        x_sq = sb.tile([Q, I], F32, name="x_sq")
        for h in range(2):
            nc.scalar.activation(x_sq[:, h * HALF : (h + 1) * HALF], neg_score[h], ACT.Square, bias=mean[:])
        root = sb.tile([Q, I], F32, name="root", tag="root", align_bytes=64)
        for h in range(2):
            cols = slice(h * HALF, (h + 1) * HALF)
            nc.scalar.activation(root[:, cols], x_sq[:, cols], ACT.Abs_reciprocal_sqrt, bias=width_sq[:])
        part = sb.tile([Q, I], F32, name="part")
        part_sum = placed.tile([Q, 1], F32, name="part_sum", offset=PLANES * PLANE_BYTES, align_bytes=64)
        nc.scalar.activation(part[:], root[:], ACT.Square, accum_out=part_sum[:])

        factor_rows = ps.tile([P, PACK, P], F32, name="factor_rows", tag="bank0")
        for t in range(PACK):
            nc.tensor.transpose(factor_rows[:, t, :], factor4[:, t : t + 1].to_broadcast([P, P]), ident[:])

        def turn(word_sets, name, bank, grouped):
            turned = ps.tile([P, 2, P], F32, name=f"{name}_turned", tag=bank)
            for u in range(2):
                nc.tensor.transpose(turned[:, u, :], word_sets[u], ident[:])
            nc.scalar.copy(
                grouped.bitcast(F32).rearrange("p (c u) -> p c u", u=2), turned[:].rearrange("p u c -> p c u")
            )

        def quantise(grouped, name, offset):
            columns = grouped.shape[1] // PACK
            codes = placed.tile([P, columns], U32, name=f"{name}_codes", offset=offset, align_bytes=64)
            scales = sb.tile([P, columns], U8, name=f"{name}_scales", align_bytes=64)
            nc.vector.quantize_mx(out=codes[:].bitcast(FP8X4), scales=scales[:], in_=grouped)
            return codes, scales

        def pick(j, pool, **place):
            picked = pool.tile([P, I], BF16, name=f"picked{j}", align_bytes=64, **place)
            nc.vector.tensor_copy(picked[:], val_planes[j][:].indirect(offsets[:]))
            words = picked[:].bitcast(F32)
            return [words[:, u : I // 2 : 2] for u in range(2)]

        picked01 = [pick(0, sb, tag="sums1"), pick(1, sb, tag="sums0")]
        grouped01 = sb.tile([P, 2 * I], BF16, name="grouped01", tag="root", align_bytes=64)
        for j in range(2):
            turn(picked01[j], f"v{j}", f"bank{5 + j}", grouped01[:, j * I : (j + 1) * I])
        picked2 = pick(2, sb)

        inv_sum = sb.tile([Q, 1], F32, name="inv_sum", tag="factor4")
        nc.vector.reciprocal(inv_sum[:], part_sum[:])
        values01 = quantise(grouped01[:], "v01", PLANES * PLANE_BYTES)
        weight_words = []
        for u in range(2):
            weight = sb.tile([Q, HALF], BF16, name=f"weight{u}", align_bytes=64)
            nc.vector.scalar_tensor_tensor(
                weight[:].rearrange("q (s r) -> q s r", r=2),
                part[:].rearrange("q (s t) -> q s t", t=PACK)[:, :, 2 * u : 2 * u + 2],
                inv_sum[:],
                factor_rows[:, 2 * u : 2 * u + 2, :].rearrange("q r s -> q s r"),
                ALU.mult,
                ALU.mult,
            )
            weight_words.append(weight[:].bitcast(F32))
        grouped_w = sb.tile([P, I], BF16, name="grouped_w", align_bytes=64)
        turn(weight_words, "w", "bank3", grouped_w[:])

        grouped2 = sb.tile([P, I], BF16, name="grouped2", align_bytes=64)
        turn(picked2, "v2", "bank3", grouped2[:])
        grouped3 = placed.tile([P, I], BF16, name="grouped3", offset=LAST_GROUPED, align_bytes=64)
        turn(pick(3, placed, offset=2 * PLANE_BYTES), "v3", "bank4", grouped3[:])
        weights = quantise(grouped_w[:], "w", 3 * PLANE_BYTES)
        values2 = quantise(grouped2[:], "v2", 3 * PLANE_BYTES + CODES_BYTES)
        values3 = quantise(grouped3[:], "v3", 3 * PLANE_BYTES + 2 * CODES_BYTES)

        def multiply(acc, values):
            nc.tensor.matmul_mx(
                out=acc,
                lhsT=weights[0][:].bitcast(FP8X4),
                lhsT_scale=weights[1][:],
                rhs=values[0][:].bitcast(FP8X4),
                rhs_scale=values[1][:],
                start=True,
                stop=True,
            )

        o01 = ps.tile([Q, PAIR], F32, name="o01", tag="bank1")
        multiply(o01[:], values01)
        o23 = []
        for values, bank in ((values2, "bank2"), (values3, "bank5")):
            o_plane = ps.tile([Q, P], F32, name=f"o_{bank}", tag=bank)
            multiply(o_plane[:], values)
            o23.append(o_plane)

        excess = sb.tile([Q, PAIR], F32, name="excess")
        nc.vector.tensor_tensor(excess[:], o01[:], floor_pairs[0][:], ALU.subtract)
        base = sb.tile([Q, PAIR], F32, name="base")
        nc.vector.scalar_tensor_tensor(base[:], o01[:], SMALL_SHARE, floor_pairs[0][:], ALU.mult, ALU.add)
        lift = sb.tile([Q, PAIR], F32, name="lift")
        nc.scalar.activation(lift[:], excess[:], ACT.Relu, scale=0.9)
        result01 = sb.tile([Q, PAIR], F32, name="result01")
        nc.gpsimd.tensor_tensor(result01[:], base[:], lift[:], ALU.add)
        nc.sync.dma_start(out[:, :PAIR], result01[:])

        floor_larger = placed.tile([Q, PAIR], F32, name="floor_larger", offset=LAST_GROUPED - I, align_bytes=64)
        o_larger = placed.tile([Q, PAIR], F32, name="o_larger", offset=LAST_GROUPED + I, align_bytes=64)
        for n, o_plane in enumerate(o23):
            cols = slice(n * P, (n + 1) * P)
            floor_plane = floor_pairs[1][:, cols]
            nc.vector.scalar_tensor_tensor(floor_larger[:, cols], o_plane[:], SMALL_SHARE, floor_plane, ALU.mult, ALU.add)
            nc.vector.scalar_tensor_tensor(o_larger[:, cols], floor_plane, SMALL_SHARE, o_plane[:], ALU.mult, ALU.add)
        result23 = sb.tile([Q, PAIR], F32, name="result23")
        nc.vector.tensor_tensor(result23[:], floor_larger[:], o_larger[:], ALU.max)
        nc.sync.dma_start(out[:, PAIR:], result23[:])
